import numpy as np
import ml_dtypes


def mxq(x, axis, fmt="e4m3"):
    dtype, down = {"e4m3": (ml_dtypes.float8_e4m3fn, 7), "e5m2": (ml_dtypes.float8_e5m2, 14)}[fmt]
    v = np.moveaxis(np.asarray(x, np.float32).astype(ml_dtypes.bfloat16).astype(np.float64), axis, -1)
    blocks = v.reshape(v.shape[:-1] + (-1, 32))
    amax = np.abs(blocks).max(-1, keepdims=True)
    byte = np.maximum(np.where(amax > 0, np.frexp(amax)[1] - 1 + 127, 0) - down, 1)
    scale = np.exp2(byte - 127.0)
    codes = (blocks / scale).astype(np.float32).astype(dtype).astype(np.float64)
    return np.moveaxis((codes * scale).reshape(v.shape), -1, axis)


WIDE = False


def mx_kscale(k):
    if not WIDE:
        return np.ones(k)
    levels = np.array([10, -10, 5, -5, 0])
    if k % 512:
        return np.exp2(np.random.permutation(np.resize(levels, k // 32))).repeat(32)
    a = np.empty((k // 512, 16))
    for p in range(k // 512):
        a[p, :8] = np.random.permutation(np.resize(levels, 8))
        for g in range(8):
            far = levels[np.abs(levels - a[p, g]) >= 10]
            a[p, g + 8] = far[np.random.randint(len(far))]
    return np.exp2(a.ravel()).repeat(32)


def f64(x):
    return np.asarray(x).astype(np.float64)


def striped(idx):
    return np.tile(idx.reshape(-1, 16).T, (8, 1)).astype(np.uint16)


def unstriped(offs):
    return offs[:16].T.reshape(-1).astype(np.int64)


def pack_weight(w):
    k, n = w.shape
    w = f64(np.asarray(w, np.float32).astype(ml_dtypes.bfloat16)).reshape(k // 32, 32, n)
    amax = np.abs(w).max(1)
    byte = np.clip(np.where(amax > 0, np.frexp(amax)[1] - 1 + 127 - 7, 1), 1, 254)
    scaled = (w * np.exp2(127.0 - byte)[:, None, :]).reshape(k, n).astype(np.float32)
    words = np.ascontiguousarray(scaled.reshape(k // 512, 128, 4, n).transpose(0, 1, 3, 2)).astype(ml_dtypes.float8_e4m3fn).view(np.uint8)
    return words, np.ascontiguousarray(byte.astype(np.uint8).reshape(k // 512, 16, n))


def unpack_weight(words, scales):
    g, p, n, _ = words.shape
    vals = np.ascontiguousarray(words).view(ml_dtypes.float8_e4m3fn).astype(np.float64) * np.repeat(np.exp2(scales.astype(np.float64) - 127.0), 8, axis=1)[..., None]
    return vals.transpose(0, 1, 3, 2).reshape(g * 512, n)


K, T, S, N = 1024, 1024, 512, 256
P = 2 ** 7


def setup_inputs():
    n = np.random.standard_normal
    s = mx_kscale(K)[:, None]
    packed_xT = pack_weight(n((K, T)) * s)
    return {
        "x_words": packed_xT[0],
        "x_scales": packed_xT[1],
        "tscale": np.tile(np.random.uniform(0.25, 2.0, T), (P, 1)).astype(np.float32),
        "cscale": np.random.uniform(0.5, 1.5, (N, 1)).astype(np.float32),
        "w1": (n((K, N)) / np.sqrt(K) / s).astype(np.float32),
        "offs": striped(np.random.permutation(T)[:S]),
    }


def reference(x_words, x_scales, tscale, cscale, w1, offs):
    xq = unpack_weight(x_words, x_scales)[:, unstriped(offs)]
    y = mxq(f64(w1), 0, "e4m3").T @ xq
    tg = f64(tscale)[:1][:, unstriped(offs)]
    return (f64(cscale) * y) * tg

@@ -1,0 +1,152 @@
+from contextlib import ExitStack
+
+import concourse.mybir as mybir
+from concourse.masks import make_identity
+
+K, T, S, N = 1024, 1024, 512, 256
+FLOPS = 2 * K * S * N
+BYTES = K * T + K // 32 * T + 4 * T + 4 * N + 4 * K * N + 2 * 128 * (S // 16) + 4 * N * S
+
+F32 = mybir.dt.float32
+BF16 = mybir.dt.bfloat16
+I32 = mybir.dt.int32
+U32 = mybir.dt.uint32
+U16 = mybir.dt.uint16
+U8 = mybir.dt.uint8
+FP8X4 = mybir.dt.float8_e4m3fn_x4
+MULT = mybir.AluOpType.mult
+
+P = 128
+PACK = 4
+K_PASS = P * PACK
+PASSES = K // K_PASS
+M_TILES = N // P
+QUADRANT = 32
+SCALE_ROWS = 4
+T_COLS = T // P
+BANK_BLOCKS = 4
+HALF = S // 2
+
+
+def tile_picked_tokscale_none_p_kernel(
+    tc, x_words, x_scales, tscale, cscale, w1, offs, out
+):
+    nc = tc.nc
+    with ExitStack() as ctx:
+        sb = ctx.enter_context(tc.tile_pool(name="sb", bufs=1))
+        ps = ctx.enter_context(tc.psum_pool(name="ps", bufs=1))
+
+        offsets = sb.tile([P, S // 16], U16, name="offsets")
+        nc.sync.dma_start(offsets[:], offs)
+
+        planes = sb.tile([P, T], U8, name="planes", align_bytes=64)
+        nc.gpsimd.memset(planes[:].bitcast(I32), 0)
+
+        t_cols = sb.tile([P, T_COLS], F32, name="t_cols", tag="head", align_bytes=64)
+        nc.sync.dma_start(t_cols[:], tscale[0].rearrange("(q c) -> q c", c=T_COLS))
+
+        for q in range(P // QUADRANT):
+            nc.sync.dma_start(
+                planes[QUADRANT * q : QUADRANT * q + PASSES * SCALE_ROWS, :].bitcast(I32),
+                x_scales[:, SCALE_ROWS * q : SCALE_ROWS * (q + 1), :].bitcast(I32),
+            )
+
+        ident = sb.tile([P, P], F32, name="ident")
+        make_identity(nc, ident[:])
+
+        def load_words(z):
+            words = sb.tile([P, T], U32, name="words%d" % z, align_bytes=64)
+            nc.sync.dma_start(
+                words[:].bitcast(I32),
+                x_words[z].rearrange("p n t -> p (n t)").bitcast(I32),
+            )
+            return words
+
+        def load_w(z, c0, c1):
+            raw = sb.tile([P, PACK, c1 - c0], F32, name="raw%d_%d" % (z, c0))
+            rows = w1[z * K_PASS : (z + 1) * K_PASS, c0:c1]
+            nc.sync.dma_start(raw[:], rows.rearrange("(p j) c -> p j c", j=PACK))
+            return raw
+
+        words0 = load_words(0)
+        raw0 = load_w(0, 0, N)
+        words1 = load_words(1)
+        raw1 = [load_w(1, m * P, (m + 1) * P) for m in range(M_TILES)]
+
+        c_cols = sb.tile([P, M_TILES], F32, name="c_cols")
+        with nc.allow_non_contiguous_dma(reason="one channel scale a partition"):
+            nc.sync.dma_start(c_cols[:], cscale.rearrange("(m p) o -> p (m o)", p=P))
+
+        t_all = sb.tile([P, T], F32, name="t_all")
+        t_view = t_all[:].rearrange("p (n h i) -> p n h i", h=T_COLS // BANK_BLOCKS, i=BANK_BLOCKS)
+        for h in range(T_COLS // BANK_BLOCKS):
+            bank = ps.tile([P, BANK_BLOCKS, P], F32, name="t_bank%d" % h)
+            for i in range(BANK_BLOCKS):
+                c = BANK_BLOCKS * h + i
+                nc.tensor.transpose(bank[:, i, :], t_cols[:, c : c + 1].to_broadcast([P, P]), ident[:])
+            nc.scalar.copy(t_view[:, :, h, :], bank[:].rearrange("p i n -> p n i"))
+
+        def round_w(raw, name, tag):
+            width = raw.shape[2]
+            grouped = sb.tile([P, width, PACK], BF16, name="grouped" + name, tag=tag, align_bytes=64)
+            nc.scalar.copy(
+                grouped[:].rearrange("p (c i) j -> p c j i", i=4),
+                raw[:].rearrange("p j (c i) -> p c j i", i=4),
+            )
+            return grouped
+
+        def quantize_w(grouped, name):
+            width = grouped.shape[1]
+            codes = sb.tile([P, width], U32, name="codes" + name, align_bytes=64)
+            scales = sb.tile([P, width], U8, name="scales" + name, align_bytes=64)
+            nc.vector.quantize_mx(
+                out=codes[:].bitcast(FP8X4),
+                scales=scales[:],
+                in_=grouped[:].rearrange("p c j -> p (c j)"),
+            )
+            return codes, scales
+
+        def gather(window, dtype, name, tag, first=0, count=S):
+            picked = sb.tile([P, count], dtype, name=name, tag=tag, align_bytes=64)
+            entries = offsets[:, first // 16 : (first + count) // 16]
+            nc.vector.tensor_copy(picked[:], window[:].indirect(entries))
+            return picked
+
+        acc = [ps.tile([P, S], F32, name="acc%d" % m) for m in range(M_TILES)]
+
+        planes_g = gather(planes, U8, "planes_g", "planes_g")
+        words0_g = gather(words0, U32, "words0_g", "words0_g")
+        t_g = [gather(t_all, F32, "t_g0", "t_g0", 0, HALF)]
+        grouped0 = round_w(raw0, "0", "head")
+        codes0, scales0 = quantize_w(grouped0, "0")
+        for m in range(M_TILES):
+            cols = slice(m * P, (m + 1) * P)
+            nc.tensor.matmul_mx(
+                out=acc[m][:],
+                lhsT=codes0[:, cols].bitcast(FP8X4),
+                lhsT_scale=scales0[:, cols],
+                rhs=words0_g[:].bitcast(FP8X4),
+                rhs_scale=planes_g[:],
+                start=True,
+                stop=False,
+            )
+        words1_g = gather(words1, U32, "words1_g", "head")
+        for m in range(M_TILES):
+            grouped1 = round_w(raw1[m], "1_%d" % m, "g1_%d" % m)
+            codes1, scales1 = quantize_w(grouped1, "1_%d" % m)
+            nc.tensor.matmul_mx(
+                out=acc[m][:],
+                lhsT=codes1[:].bitcast(FP8X4),
+                lhsT_scale=scales1[:],
+                rhs=words1_g[:].bitcast(FP8X4),
+                rhs_scale=planes_g[SCALE_ROWS:P, :],
+                start=False,
+                stop=True,
+            )
+        t_g.append(gather(t_all, F32, "t_g1", "g1_%d" % (M_TILES - 1), HALF, HALF))
+        for m in range(M_TILES):
+            for h in range(S // HALF):
+                cols = slice(h * HALF, (h + 1) * HALF)
+                result = sb.tile([P, HALF], F32, name="result%d_%d" % (m, h))
+                nc.vector.scalar_tensor_tensor(result[:], acc[m][:, cols], c_cols[:, m : m + 1], t_g[h][:], MULT, MULT)
+                nc.sync.dma_start(out[m * P : (m + 1) * P, cols], result[:])

@@ -51,7 +51,7 @@ def tile_picked_tokscale_none_p_kernel(
                 x_scales[:, SCALE_ROWS * q : SCALE_ROWS * (q + 1), :].bitcast(I32),
             )
 
-        ident = sb.tile([P, P], F32, name="ident")
+        ident = sb.tile([P, P], F32, name="ident", tag="tail0", align_bytes=64)
         make_identity(nc, ident[:])
 
         def load_words(z):
@@ -62,16 +62,16 @@ def tile_picked_tokscale_none_p_kernel(
             )
             return words
 
-        def load_w(z, c0, c1):
-            raw = sb.tile([P, PACK, c1 - c0], F32, name="raw%d_%d" % (z, c0))
-            rows = w1[z * K_PASS : (z + 1) * K_PASS, c0:c1]
+        def load_w(z, tag):
+            raw = sb.tile([P, PACK, N], F32, name="raw%d" % z, tag=tag, align_bytes=64)
+            rows = w1[z * K_PASS : (z + 1) * K_PASS, :]
             nc.sync.dma_start(raw[:], rows.rearrange("(p j) c -> p j c", j=PACK))
             return raw
 
         words0 = load_words(0)
-        raw0 = load_w(0, 0, N)
+        raw0 = load_w(0, "tail1")
+        raw1 = load_w(1, "raw1")
         words1 = load_words(1)
-        raw1 = [load_w(1, m * P, (m + 1) * P) for m in range(M_TILES)]
 
         c_cols = sb.tile([P, M_TILES], F32, name="c_cols")
         with nc.allow_non_contiguous_dma(reason="one channel scale a partition"):
@@ -86,12 +86,11 @@ def tile_picked_tokscale_none_p_kernel(
                 nc.tensor.transpose(bank[:, i, :], t_cols[:, c : c + 1].to_broadcast([P, P]), ident[:])
             nc.scalar.copy(t_view[:, :, h, :], bank[:].rearrange("p i n -> p n i"))
 
-        def round_w(raw, name, tag):
-            width = raw.shape[2]
-            grouped = sb.tile([P, width, PACK], BF16, name="grouped" + name, tag=tag, align_bytes=64)
+        def round_w(raw, c0, c1, name, tag):
+            grouped = sb.tile([P, c1 - c0, PACK], BF16, name="grouped" + name, tag=tag, align_bytes=64)
             nc.scalar.copy(
                 grouped[:].rearrange("p (c i) j -> p c j i", i=4),
-                raw[:].rearrange("p j (c i) -> p c j i", i=4),
+                raw[:, :, c0:c1].rearrange("p j (c i) -> p c j i", i=4),
             )
             return grouped
 
@@ -106,47 +105,48 @@ def tile_picked_tokscale_none_p_kernel(
             )
             return codes, scales
 
-        def gather(window, dtype, name, tag, first=0, count=S):
+        def gather(window, dtype, first, count, name, tag):
             picked = sb.tile([P, count], dtype, name=name, tag=tag, align_bytes=64)
             entries = offsets[:, first // 16 : (first + count) // 16]
             nc.vector.tensor_copy(picked[:], window[:].indirect(entries))
             return picked
 
-        acc = [ps.tile([P, S], F32, name="acc%d" % m) for m in range(M_TILES)]
+        acc = [[ps.tile([P, HALF], F32, name="acc%d_%d" % (h, m)) for m in range(M_TILES)] for h in range(S // HALF)]
 
-        planes_g = gather(planes, U8, "planes_g", "planes_g")
-        words0_g = gather(words0, U32, "words0_g", "words0_g")
-        t_g = [gather(t_all, F32, "t_g0", "t_g0", 0, HALF)]
-        grouped0 = round_w(raw0, "0", "head")
-        codes0, scales0 = quantize_w(grouped0, "0")
-        for m in range(M_TILES):
-            cols = slice(m * P, (m + 1) * P)
+        def multiply(z, h, m, codes, scales, picked):
             nc.tensor.matmul_mx(
-                out=acc[m][:],
-                lhsT=codes0[:, cols].bitcast(FP8X4),
-                lhsT_scale=scales0[:, cols],
-                rhs=words0_g[:].bitcast(FP8X4),
-                rhs_scale=planes_g[:],
-                start=True,
-                stop=False,
+                out=acc[h][m][:],
+                lhsT=codes.bitcast(FP8X4),
+                lhsT_scale=scales,
+                rhs=picked.bitcast(FP8X4),
+                rhs_scale=planes_g[SCALE_ROWS * z : P, h * HALF : (h + 1) * HALF],
+                start=(z == 0),
+                stop=(z == PASSES - 1),
             )
-        words1_g = gather(words1, U32, "words1_g", "head")
-        for m in range(M_TILES):
-            grouped1 = round_w(raw1[m], "1_%d" % m, "g1_%d" % m)
-            codes1, scales1 = quantize_w(grouped1, "1_%d" % m)
-            nc.tensor.matmul_mx(
-                out=acc[m][:],
-                lhsT=codes1[:].bitcast(FP8X4),
-                lhsT_scale=scales1[:],
-                rhs=words1_g[:].bitcast(FP8X4),
-                rhs_scale=planes_g[SCALE_ROWS:P, :],
-                start=False,
-                stop=True,
-            )
-        t_g.append(gather(t_all, F32, "t_g1", "g1_%d" % (M_TILES - 1), HALF, HALF))
-        for m in range(M_TILES):
-            for h in range(S // HALF):
-                cols = slice(h * HALF, (h + 1) * HALF)
-                result = sb.tile([P, HALF], F32, name="result%d_%d" % (m, h))
-                nc.vector.scalar_tensor_tensor(result[:], acc[m][:, cols], c_cols[:, m : m + 1], t_g[h][:], MULT, MULT)
-                nc.sync.dma_start(out[m * P : (m + 1) * P, cols], result[:])
+
+        planes_g = gather(planes, U8, 0, S, "planes_g", "planes_g")
+        words0_g = gather(words0, U32, 0, S, "words0_g", "words0_g")
+        t_g = gather(t_all, F32, 0, S, "t_g", "t_g")
+
+        codes0, scales0 = quantize_w(round_w(raw0, 0, N, "0", "head"), "0")
+        for h in range(S // HALF):
+            for m in range(M_TILES):
+                cols = slice(m * P, (m + 1) * P)
+                multiply(0, h, m, codes0[:, cols], scales0[:, cols], words0_g[:, h * HALF : (h + 1) * HALF])
+
+        quantized1 = []
+        words1_g = []
+        for i in range(M_TILES):
+            grouped = round_w(raw1, i * P, (i + 1) * P, "1_%d" % i, "tail%d" % i)
+            quantized1.append(quantize_w(grouped, "1_%d" % i))
+            words1_g.append(gather(words1, U32, i * HALF, HALF, "words1_g%d" % i, "tail%d" % i))
+        for h in range(S // HALF):
+            for m in range(M_TILES):
+                codes1, scales1 = quantized1[m]
+                multiply(1, h, m, codes1[:], scales1[:], words1_g[h][:])
+        for h in range(S // HALF):
+            tokens = slice(h * HALF, (h + 1) * HALF)
+            for m in range(M_TILES):
+                result = sb.tile([P, HALF], F32, name="result%d_%d" % (h, m))
+                nc.vector.scalar_tensor_tensor(result[:], acc[h][m][:], c_cols[:, m : m + 1], t_g[:, tokens], MULT, MULT)
+                nc.sync.dma_start(out[m * P : (m + 1) * P, tokens], result[:])

@@ -26,6 +26,7 @@ SCALE_ROWS = 4
 T_COLS = T // P
 BANK_BLOCKS = 4
 HALF = S // 2
+BLOCK_WORDS = 8
 
 
 def tile_picked_tokscale_none_p_kernel(
@@ -73,9 +74,9 @@ def tile_picked_tokscale_none_p_kernel(
         raw1 = load_w(1, "raw1")
         words1 = load_words(1)
 
-        c_cols = sb.tile([P, M_TILES], F32, name="c_cols")
+        c_cols = sb.tile([P, M_TILES, BLOCK_WORDS], F32, name="c_cols")
         with nc.allow_non_contiguous_dma(reason="one channel scale a partition"):
-            nc.sync.dma_start(c_cols[:], cscale.rearrange("(m p) o -> p (m o)", p=P))
+            nc.sync.dma_start(c_cols[:, :, 0:1], cscale.rearrange("(m p) o -> p m o", p=P))
 
         t_all = sb.tile([P, T], F32, name="t_all")
         t_view = t_all[:].rearrange("p (n h i) -> p n h i", h=T_COLS // BANK_BLOCKS, i=BANK_BLOCKS)
@@ -86,22 +87,19 @@ def tile_picked_tokscale_none_p_kernel(
                 nc.tensor.transpose(bank[:, i, :], t_cols[:, c : c + 1].to_broadcast([P, P]), ident[:])
             nc.scalar.copy(t_view[:, :, h, :], bank[:].rearrange("p i n -> p n i"))
 
-        def round_w(raw, c0, c1, name, tag):
-            grouped = sb.tile([P, c1 - c0, PACK], BF16, name="grouped" + name, tag=tag, align_bytes=64)
+        def round_w(grouped, raw):
             nc.scalar.copy(
-                grouped[:].rearrange("p (c i) j -> p c j i", i=4),
-                raw[:, :, c0:c1].rearrange("p j (c i) -> p c j i", i=4),
+                grouped.rearrange("p (c i) j -> p c j i", i=4),
+                raw.rearrange("p j (c i) -> p c j i", i=4),
             )
-            return grouped
 
         def quantize_w(grouped, name):
-            width = grouped.shape[1]
-            codes = sb.tile([P, width], U32, name="codes" + name, align_bytes=64)
-            scales = sb.tile([P, width], U8, name="scales" + name, align_bytes=64)
+            codes = sb.tile([P, P], U32, name="codes" + name, align_bytes=64)
+            scales = sb.tile([P, P], U8, name="scales" + name, align_bytes=64)
             nc.vector.quantize_mx(
                 out=codes[:].bitcast(FP8X4),
                 scales=scales[:],
-                in_=grouped[:].rearrange("p c j -> p (c j)"),
+                in_=grouped.rearrange("p c j -> p (c j)"),
             )
             return codes, scales
 
@@ -128,17 +126,20 @@ def tile_picked_tokscale_none_p_kernel(
         words0_g = gather(words0, U32, 0, S, "words0_g", "words0_g")
         t_g = gather(t_all, F32, 0, S, "t_g", "t_g")
 
-        codes0, scales0 = quantize_w(round_w(raw0, 0, N, "0", "head"), "0")
-        for h in range(S // HALF):
-            for m in range(M_TILES):
-                cols = slice(m * P, (m + 1) * P)
-                multiply(0, h, m, codes0[:, cols], scales0[:, cols], words0_g[:, h * HALF : (h + 1) * HALF])
+        grouped0 = sb.tile([P, N, PACK], BF16, name="grouped0", tag="head", align_bytes=64)
+        for m in range(M_TILES):
+            cols = slice(m * P, (m + 1) * P)
+            round_w(grouped0[:, cols, :], raw0[:, :, cols])
+            codes0, scales0 = quantize_w(grouped0[:, cols, :], "0_%d" % m)
+            for h in range(S // HALF):
+                multiply(0, h, m, codes0[:], scales0[:], words0_g[:, h * HALF : (h + 1) * HALF])
 
         quantized1 = []
         words1_g = []
         for i in range(M_TILES):
-            grouped = round_w(raw1, i * P, (i + 1) * P, "1_%d" % i, "tail%d" % i)
-            quantized1.append(quantize_w(grouped, "1_%d" % i))
+            grouped1 = sb.tile([P, P, PACK], BF16, name="grouped1_%d" % i, tag="tail%d" % i, align_bytes=64)
+            round_w(grouped1[:], raw1[:, :, i * P : (i + 1) * P])
+            quantized1.append(quantize_w(grouped1[:], "1_%d" % i))
             words1_g.append(gather(words1, U32, i * HALF, HALF, "words1_g%d" % i, "tail%d" % i))
         for h in range(S // HALF):
             for m in range(M_TILES):
@@ -148,5 +149,5 @@ def tile_picked_tokscale_none_p_kernel(
             tokens = slice(h * HALF, (h + 1) * HALF)
             for m in range(M_TILES):
                 result = sb.tile([P, HALF], F32, name="result%d_%d" % (h, m))
-                nc.vector.scalar_tensor_tensor(result[:], acc[h][m][:], c_cols[:, m : m + 1], t_g[:, tokens], MULT, MULT)
+                nc.vector.scalar_tensor_tensor(result[:], acc[h][m][:], c_cols[:, m, 0:1], t_g[:, tokens], MULT, MULT)
                 nc.sync.dma_start(out[m * P : (m + 1) * P, tokens], result[:])

from contextlib import ExitStack

import concourse.mybir as mybir
from concourse.masks import make_identity

K, T, S, N = 1024, 1024, 512, 256
FLOPS = 2 * K * S * N
BYTES = K * T + K // 32 * T + 4 * T + 4 * N + 4 * K * N + 2 * 128 * (S // 16) + 4 * N * S

F32 = mybir.dt.float32
BF16 = mybir.dt.bfloat16
I32 = mybir.dt.int32
U32 = mybir.dt.uint32
U16 = mybir.dt.uint16
U8 = mybir.dt.uint8
FP8X4 = mybir.dt.float8_e4m3fn_x4
MULT = mybir.AluOpType.mult

P = 128
PACK = 4
K_PASS = P * PACK
PASSES = K // K_PASS
M_TILES = N // P
QUADRANT = 32
SCALE_ROWS = 4
T_COLS = T // P
BANK_BLOCKS = 4
HALF = S // 2
BLOCK_WORDS = 8


def tile_picked_tokscale_none_p_kernel(
    tc, x_words, x_scales, tscale, cscale, w1, offs, out
):
    nc = tc.nc
    with ExitStack() as ctx:
        sb = ctx.enter_context(tc.tile_pool(name="sb", bufs=1))
        ps = ctx.enter_context(tc.psum_pool(name="ps", bufs=1))

        offsets = sb.tile([P, S // 16], U16, name="offsets")
        nc.sync.dma_start(offsets[:], offs)

        planes = sb.tile([P, T], U8, name="planes", align_bytes=64)
        nc.gpsimd.memset(planes[:].bitcast(I32), 0)

        t_cols = sb.tile([P, T_COLS], F32, name="t_cols", tag="head", align_bytes=64)
        nc.sync.dma_start(t_cols[:], tscale[0].rearrange("(q c) -> q c", c=T_COLS))

        for q in range(P // QUADRANT):
            nc.sync.dma_start(
                planes[QUADRANT * q : QUADRANT * q + PASSES * SCALE_ROWS, :].bitcast(I32),
                x_scales[:, SCALE_ROWS * q : SCALE_ROWS * (q + 1), :].bitcast(I32),
            )

        ident = sb.tile([P, P], F32, name="ident", tag="tail0", align_bytes=64)
        make_identity(nc, ident[:])

        def load_words(z):
            words = sb.tile([P, T], U32, name="words%d" % z, align_bytes=64)
            nc.sync.dma_start(
                words[:].bitcast(I32),
                x_words[z].rearrange("p n t -> p (n t)").bitcast(I32),
            )
            return words

        def load_w(z, tag):
            raw = sb.tile([P, PACK, N], F32, name="raw%d" % z, tag=tag, align_bytes=64)
            rows = w1[z * K_PASS : (z + 1) * K_PASS, :]
            nc.sync.dma_start(raw[:], rows.rearrange("(p j) c -> p j c", j=PACK))
            return raw

        words0 = load_words(0)
        raw0 = load_w(0, "tail1")
        raw1 = load_w(1, "raw1")
        words1 = load_words(1)

        c_cols = sb.tile([P, M_TILES, BLOCK_WORDS], F32, name="c_cols")
        with nc.allow_non_contiguous_dma(reason="one channel scale a partition"):
            nc.sync.dma_start(c_cols[:, :, 0:1], cscale.rearrange("(m p) o -> p m o", p=P))

        t_all = sb.tile([P, T], F32, name="t_all")
        t_view = t_all[:].rearrange("p (n h i) -> p n h i", h=T_COLS // BANK_BLOCKS, i=BANK_BLOCKS)
        for h in range(T_COLS // BANK_BLOCKS):
            bank = ps.tile([P, BANK_BLOCKS, P], F32, name="t_bank%d" % h)
            for i in range(BANK_BLOCKS):
                c = BANK_BLOCKS * h + i
                nc.tensor.transpose(bank[:, i, :], t_cols[:, c : c + 1].to_broadcast([P, P]), ident[:])
            nc.scalar.copy(t_view[:, :, h, :], bank[:].rearrange("p i n -> p n i"))

        def round_w(grouped, raw):
            nc.scalar.copy(
                grouped.rearrange("p (c i) j -> p c j i", i=4),
                raw.rearrange("p j (c i) -> p c j i", i=4),
            )

        def quantize_w(grouped, name):
            codes = sb.tile([P, P], U32, name="codes" + name, align_bytes=64)
            scales = sb.tile([P, P], U8, name="scales" + name, align_bytes=64)
            nc.vector.quantize_mx(
                out=codes[:].bitcast(FP8X4),
                scales=scales[:],
                in_=grouped.rearrange("p c j -> p (c j)"),
            )
            return codes, scales

        def gather(window, dtype, first, count, name, tag):
            picked = sb.tile([P, count], dtype, name=name, tag=tag, align_bytes=64)
            entries = offsets[:, first // 16 : (first + count) // 16]
            nc.vector.tensor_copy(picked[:], window[:].indirect(entries))
            return picked

        acc = [[ps.tile([P, HALF], F32, name="acc%d_%d" % (h, m)) for m in range(M_TILES)] for h in range(S // HALF)]

        def multiply(z, h, m, codes, scales, picked):
            nc.tensor.matmul_mx(
                out=acc[h][m][:],
                lhsT=codes.bitcast(FP8X4),
                lhsT_scale=scales,
                rhs=picked.bitcast(FP8X4),
                rhs_scale=planes_g[SCALE_ROWS * z : P, h * HALF : (h + 1) * HALF],
                start=(z == 0),
                stop=(z == PASSES - 1),
            )

        planes_g = gather(planes, U8, 0, S, "planes_g", "planes_g")
        words0_g = gather(words0, U32, 0, S, "words0_g", "words0_g")
        t_g = gather(t_all, F32, 0, S, "t_g", "t_g")

        grouped0 = sb.tile([P, N, PACK], BF16, name="grouped0", tag="head", align_bytes=64)
        for m in range(M_TILES):
            cols = slice(m * P, (m + 1) * P)
            round_w(grouped0[:, cols, :], raw0[:, :, cols])
            codes0, scales0 = quantize_w(grouped0[:, cols, :], "0_%d" % m)
            for h in range(S // HALF):
                multiply(0, h, m, codes0[:], scales0[:], words0_g[:, h * HALF : (h + 1) * HALF])

        quantized1 = []
        words1_g = []
        for i in range(M_TILES):
            grouped1 = sb.tile([P, P, PACK], BF16, name="grouped1_%d" % i, tag="tail%d" % i, align_bytes=64)
            round_w(grouped1[:], raw1[:, :, i * P : (i + 1) * P])
            quantized1.append(quantize_w(grouped1[:], "1_%d" % i))
            words1_g.append(gather(words1, U32, i * HALF, HALF, "words1_g%d" % i, "tail%d" % i))
        for h in range(S // HALF):
            for m in range(M_TILES):
                codes1, scales1 = quantized1[m]
                multiply(1, h, m, codes1[:], scales1[:], words1_g[h][:])
        for h in range(S // HALF):
            tokens = slice(h * HALF, (h + 1) * HALF)
            for m in range(M_TILES):
                result = sb.tile([P, HALF], F32, name="result%d_%d" % (h, m))
                nc.vector.scalar_tensor_tensor(result[:], acc[h][m][:], c_cols[:, m, 0:1], t_g[:, tokens], MULT, MULT)
                nc.sync.dma_start(out[m * P : (m + 1) * P, tokens], result[:])
